import numpy as np
import ml_dtypes


def mxq(x, axis, fmt="e4m3"):
    dtype, down = {"e4m3": (ml_dtypes.float8_e4m3fn, 7), "e5m2": (ml_dtypes.float8_e5m2, 14)}[fmt]
    v = np.moveaxis(np.asarray(x, np.float32).astype(ml_dtypes.bfloat16).astype(np.float64), axis, -1)
    blocks = v.reshape(v.shape[:-1] + (-1, 32))
    amax = np.abs(blocks).max(-1, keepdims=True)
    byte = np.maximum(np.where(amax > 0, np.frexp(amax)[1] - 1 + 127, 0) - down, 1)
    scale = np.exp2(byte - 127.0)
    codes = (blocks / scale).astype(np.float32).astype(dtype).astype(np.float64)
    return np.moveaxis((codes * scale).reshape(v.shape), -1, axis)


WIDE = False


def mx_kscale(k):
    if not WIDE:
        return np.ones(k)
    levels = np.array([10, -10, 5, -5, 0])
    if k % 512:
        return np.exp2(np.random.permutation(np.resize(levels, k // 32))).repeat(32)
    a = np.empty((k // 512, 16))
    for p in range(k // 512):
        a[p, :8] = np.random.permutation(np.resize(levels, 8))
        for g in range(8):
            far = levels[np.abs(levels - a[p, g]) >= 10]
            a[p, g + 8] = far[np.random.randint(len(far))]
    return np.exp2(a.ravel()).repeat(32)


def f64(x):
    return np.asarray(x).astype(np.float64)


def striped(idx):
    return np.tile(idx.reshape(-1, 16).T, (8, 1)).astype(np.uint16)


def unstriped(offs):
    return offs[:16].T.reshape(-1).astype(np.int64)


E2M1 = np.array([0.0, 0.5, 1.0, 1.5, 2.0, 3.0, 4.0, 6.0, -0.0, -0.5, -1.0, -1.5, -2.0, -3.0, -4.0, -6.0])


def pack_weight(w, fmt):
    k, n = w.shape
    w = f64(np.asarray(w, np.float32).astype(ml_dtypes.bfloat16)).reshape(k // 32, 32, n)
    amax = np.abs(w).max(1)
    if fmt == "e4m3":
        byte = np.frexp(amax)[1] - 1 + 127 - 7
    else:
        mant, ex = np.frexp(amax / 6.0)
        byte = np.where(mant > 0.5, ex, ex - 1) + 127
    byte = np.clip(np.where(amax > 0, byte, 1), 1, 254)
    scaled = (w * np.exp2(127.0 - byte)[:, None, :]).reshape(k, n).astype(np.float32)
    by_word = np.ascontiguousarray(scaled.reshape(k // 512, 128, 4, n).transpose(0, 1, 3, 2))
    if fmt == "e4m3":
        words = by_word.astype(ml_dtypes.float8_e4m3fn).view(np.uint8)
    else:
        c = by_word.astype(ml_dtypes.float4_e2m1fn).view(np.uint8) & 0xF
        words = (c[..., 0::2] | (c[..., 1::2] << 4)).reshape(k // 512, 128, 2 * n)
    return np.ascontiguousarray(words), np.ascontiguousarray(byte.astype(np.uint8).reshape(k // 512, 16, n))


def unpack_weight(words, scales, fmt):
    g, _, n = scales.shape
    words = np.ascontiguousarray(words).reshape(g, 128, n, -1)
    if fmt == "e4m3":
        vals = words.view(ml_dtypes.float8_e4m3fn).astype(np.float64)
    else:
        nib = np.empty((g, 128, n, 4), np.uint8)
        nib[..., 0::2] = words & 0xF
        nib[..., 1::2] = words >> 4
        vals = E2M1[nib]
    vals = vals * np.repeat(np.exp2(scales.astype(np.float64) - 127.0), 8, axis=1)[..., None]
    return vals.transpose(0, 1, 3, 2).reshape(g * 512, n)


def gelu(v):
    return 0.5 * v * (1.0 + np.tanh(np.sqrt(2.0 / np.pi) * (v + 0.044715 * v**3)))


K, H, T, S, T2, T3, S2, P = 1024, 512, 4096, 1024, 2048, 2048, 1024, 512

def setup_inputs():
    n = np.random.standard_normal
    s = mx_kscale(K)[:, None]
    u = mx_kscale(H)[:, None]
    tab_words, tab_scales = pack_weight(n((K, T)) * s, "e4m3")
    tab2_words, tab2_scales = pack_weight(n((H, T3)) / np.sqrt(H) / u, "e4m3")
    w4_words, w4_scales = pack_weight(n((K, H)) / np.sqrt(K) / s * u.T, "e2m1")
    return {
        "tab_words": tab_words, "tab_scales": tab_scales,
        "tab2_words": tab2_words, "tab2_scales": tab2_scales,
        "offs": striped(np.random.permutation(T)[:S]),
        "offs2": striped(np.random.permutation(T3)[:S2]),
        "offs3": striped(np.random.permutation(T2)[:S]),
        "offs4": striped(np.random.permutation(T2)[:P]),
        "w1": (n((K, H)) / np.sqrt(K) / s * u.T).astype(np.float32),
        "b1": ((0.7 * n(H) - 0.5) * u[:, 0]).astype(np.float32),
        "w4_words": w4_words, "w4_scales": w4_scales,
        "page0": (n((H, T2)) * u).astype(np.float32),
        "wgs": np.exp(0.3 * n((128, S))).astype(np.float32),
        "lic": (0.8 * n((S2, P))).astype(np.float32),
    }

def reference(tab_words, tab_scales, tab2_words, tab2_scales, offs, offs2, offs3, offs4,
              w1, b1, w4_words, w4_scales, page0, wgs, lic):
    v = unpack_weight(tab_words, tab_scales, "e4m3")[:, unstriped(offs)]
    v2 = unpack_weight(tab2_words, tab2_scales, "e4m3")[:, unstriped(offs2)]
    w4 = unpack_weight(w4_words, w4_scales, "e2m1")
    a1 = (mxq(f64(w1), 0, "e4m3").T @ v) + f64(b1)[:, None]
    a2 = w4.T @ v
    h = np.maximum(a1, a2)
    page = f64(page0).copy()
    page[:, unstriped(offs3)] = np.tile(f64(wgs), (H // 128, 1)) * h
    x = np.abs(page[:, unstriped(offs4)])
    e = v2.T @ mxq(x, 0, "e4m3")
    return np.tanh(e + f64(lic))

@@ -1,0 +1,230 @@
+from contextlib import ExitStack
+
+import concourse.mybir as mybir
+
+K, H, T, S, T2, T3, S2, OPENED = 1024, 512, 4096, 1024, 2048, 2048, 1024, 512
+FLOPS = 2 * (2 * K * H * S + H * S2 * OPENED)
+
+F32 = mybir.dt.float32
+BF16 = mybir.dt.bfloat16
+I32 = mybir.dt.int32
+U32 = mybir.dt.uint32
+U16 = mybir.dt.uint16
+U8 = mybir.dt.uint8
+FP8X4 = mybir.dt.float8_e4m3fn_x4
+FP4X4 = mybir.dt.float4_e2m1fn_x4
+ALU = mybir.AluOpType
+ACT = mybir.ActivationFunctionType
+
+P = 128
+PACK = 4
+PASSES = K // (P * PACK)
+QUADS = 4
+ROWS = 4
+BANK = 512
+HALF = OPENED // 2
+
+
+def tile_list_lightbox_candidate_scores_kernel(
+    tc, tab_words, tab_scales, tab2_words, tab2_scales, offs, offs2, offs3, offs4,
+    w1, b1, w4_words, w4_scales, page0, wgs, lic, out,
+):
+    nc = tc.nc
+    with ExitStack() as ctx:
+        keep = ctx.enter_context(tc.tile_pool(name="keep", bufs=1))
+        ring = ctx.enter_context(tc.tile_pool(name="ring", bufs=2))
+        psum = ctx.enter_context(tc.psum_pool(name="psum", bufs=8))
+
+        def held(shape, dtype, name):
+            return keep.tile(shape, dtype, name=name, align_bytes=64)
+
+        list1 = keep.tile([P, S // 16], U16, name="list1")
+        list2 = keep.tile([P, S2 // 16], U16, name="list2")
+        list3 = keep.tile([P, S // 16], U16, name="list3")
+        list4 = keep.tile([P, OPENED // 16], U16, name="list4")
+
+        tab_scale_rows = held([P, T], U8, "tab_scale_rows")
+        tab2_scale_rows = held([P, T3], U8, "tab2_scale_rows")
+        w4_scale_rows = held([P, H], U8, "w4_scale_rows")
+        plane_widths = [S + H, S + H + S2]
+        planes = [held([P, plane_widths[a]], U8, f"planes{a}") for a in range(PASSES)]
+        v_scales = [planes[a][:, 0:S] for a in range(PASSES)]
+        w4_scale = [planes[a][:, S : S + H] for a in range(PASSES)]
+        v2_scales = planes[1][:, S + H : S + H + S2]
+        first_row = P - PASSES * 16
+        first_row2 = P - 16
+        nc.vector.memset(tab_scale_rows[0:first_row, :].bitcast(I32), 0)
+        nc.vector.memset(w4_scale_rows[0:first_row, :].bitcast(I32), 0)
+        nc.vector.memset(tab2_scale_rows[0:first_row2, :].bitcast(I32), 0)
+        for a in range(PASSES):
+            nc.vector.memset(planes[a][:].bitcast(I32), 0)
+
+        nc.sync.dma_start(list1[:], offs)
+        nc.sync.dma_start(
+            tab_scale_rows[first_row:P, :].bitcast(I32),
+            tab_scales.rearrange("a q t -> (a q) t").bitcast(I32),
+        )
+        nc.sync.dma_start(
+            w4_scale_rows[first_row:P, :].bitcast(I32),
+            w4_scales.rearrange("a q c -> (a q) c").bitcast(I32),
+        )
+        nc.sync.dma_start(list2[:], offs2)
+        nc.sync.dma_start(tab2_scale_rows[first_row2:P, :].bitcast(I32), tab2_scales[0].bitcast(I32))
+        w1_raw = [held([P, PACK, H], F32, f"w1_raw{a}") for a in range(PASSES)]
+        for a in range(PASSES):
+            nc.sync.dma_start(
+                w1_raw[a][:], w1[a * P * PACK : (a + 1) * P * PACK, :].rearrange("(p j) c -> p j c", j=PACK)
+            )
+        w4_raw = held([P, PASSES, 2 * H], U8, "w4_raw")
+        nc.sync.dma_start(w4_raw[:].bitcast(I32), w4_words.rearrange("a p n -> p a n").bitcast(I32))
+        table = [held([P, T], U32, f"table{a}") for a in range(PASSES)]
+        for a in range(PASSES):
+            nc.sync.dma_start(
+                table[a][:].bitcast(I32), tab_words[a].rearrange("p t i -> p (t i)").bitcast(I32)
+            )
+        nc.sync.dma_start(list3[:], offs3)
+        bias = keep.tile([P, PACK], F32, name="bias")
+        nc.sync.dma_start(bias[:], b1.rearrange("(p t) -> p t", t=PACK))
+        page = [held([P, T2], F32, f"page{t}") for t in range(PACK)]
+        page_rows = page0.rearrange("(p t) c -> t p c", t=PACK)
+        nc.sync.dma_start(page[0][:], page_rows[0])
+        gain_first = keep.tile([P, S], F32, name="gain_first", tag="gain_then_v2", align_bytes=64)
+        gain_rest = held([P, PACK - 1, S], F32, "gain_rest")
+        wgs_rows = wgs.rearrange("(p t) j -> p t j", t=PACK)
+        for q in range(QUADS):
+            nc.sync.dma_start(gain_first[32 * q : 32 * (q + 1), :], wgs_rows[:, 0, :])
+        table2 = held([P, T3], U32, "table2")
+        nc.sync.dma_start(table2[:].bitcast(I32), tab2_words[0].rearrange("p t i -> p (t i)").bitcast(I32))
+        nc.sync.dma_start(page[1][:], page_rows[1])
+        for q in range(QUADS):
+            nc.sync.dma_start(gain_rest[32 * q : 32 * (q + 1), :, :], wgs_rows[:, 1:PACK, :])
+        nc.sync.dma_start(list4[:], offs4)
+        for t in range(2, PACK):
+            nc.sync.dma_start(page[t][:], page_rows[t])
+        score = held([P, S2 // P, OPENED], F32, "score")
+        nc.sync.dma_start(score[:], lic.rearrange("(i p) j -> p i j", p=P))
+
+        staged = held([P, S + H + S2], U8, "staged")
+
+        def deal_rows(a):
+            for q in range(QUADS):
+                row = first_row + 16 * a + ROWS * q
+                nc.gpsimd.dma_start(
+                    planes[a][32 * q : 32 * q + ROWS, :].bitcast(I32),
+                    staged[row : row + ROWS, 0 : plane_widths[a]].bitcast(I32),
+                )
+
+        picked_scales = held([P, S], U8, "picked_scales")
+        nc.vector.tensor_copy(picked_scales[:], tab_scale_rows[:].indirect(list1[:]))
+        nc.vector.tensor_copy(
+            staged[:, S : S + H].rearrange("p (t m) -> p t m", t=PACK),
+            w4_scale_rows[:].rearrange("p (m t) -> p t m", t=PACK),
+        )
+        nc.vector.tensor_copy(staged[:, 0:S].bitcast(I32), picked_scales[:].bitcast(I32))
+        deal_rows(0)
+        picked_scales2 = held([P, S2], U8, "picked_scales2")
+        nc.vector.tensor_copy(picked_scales2[:], tab2_scale_rows[:].indirect(list2[:]))
+        nc.vector.tensor_copy(staged[:, S + H : S + H + S2].bitcast(I32), picked_scales2[:].bitcast(I32))
+        deal_rows(1)
+
+        w1_bf16 = [held([P, H * PACK], BF16, f"w1_bf16{a}") for a in range(PASSES)]
+        for a in range(PASSES):
+            nc.scalar.copy(
+                w1_bf16[a][:].rearrange("p (t m j) -> p m t j", t=PACK, j=PACK),
+                w1_raw[a][:].rearrange("p j (m t) -> p m t j", t=PACK),
+            )
+        w4_codes = held([P, PASSES, 2 * H], U8, "w4_codes")
+        nc.vector.tensor_copy(
+            w4_codes[:].bitcast(U16).rearrange("p a (t m) -> p a t m", t=PACK),
+            w4_raw[:].bitcast(U16).rearrange("p a (m t) -> p a t m", t=PACK),
+        )
+        w1_codes = [held([P, H], U32, f"w1_codes{a}") for a in range(PASSES)]
+        w1_scale = [held([P, H], U8, f"w1_scale{a}") for a in range(PASSES)]
+        for a in range(PASSES):
+            nc.vector.quantize_mx(out=w1_codes[a][:].bitcast(FP8X4), scales=w1_scale[a][:], in_=w1_bf16[a][:])
+
+        v_codes = [held([P, S], U32, f"v_codes{a}") for a in range(PASSES)]
+        nc.vector.tensor_copy(v_codes[0][:], table[0][:].indirect(list1[:]))
+        for u in range(S // BANK):
+            nc.vector.tensor_copy(
+                v_codes[1][:, u * BANK : (u + 1) * BANK],
+                table[1][:].indirect(list1[:, u * BANK // 16 : (u + 1) * BANK // 16]),
+            )
+
+        picked = [[held([P, 2, HALF], F32, f"picked{pair}{u}") for u in range(2)] for pair in range(2)]
+        x_bf16 = [held([P, HALF, PACK], BF16, f"x_bf16{u}") for u in range(2)]
+
+        def readings(t):
+            h = ring.tile([P, S], F32, name="h")
+            rows = slice(t * P, (t + 1) * P)
+            for u in range(S // BANK):
+                cols = slice(u * BANK, (u + 1) * BANK)
+                first = psum.tile([P, BANK], F32, name="bank")
+                second = psum.tile([P, BANK], F32, name="bank")
+                for a in range(PASSES):
+                    moving = dict(
+                        rhs=v_codes[a][:, cols].bitcast(FP8X4), rhs_scale=v_scales[a][:, cols],
+                        start=a == 0, stop=a == PASSES - 1,
+                    )
+                    nc.tensor.matmul_mx(
+                        out=first[:], lhsT=w1_codes[a][:, rows].bitcast(FP8X4),
+                        lhsT_scale=w1_scale[a][:, rows], **moving,
+                    )
+                    nc.tensor.matmul_mx(
+                        out=second[:], lhsT=w4_codes[:, a, 2 * t * P : 2 * (t + 1) * P].bitcast(FP4X4),
+                        lhsT_scale=w4_scale[a][:, rows], **moving,
+                    )
+                biased = ring.tile([P, BANK], F32, name="biased")
+                nc.scalar.activation(biased[:], first[:], ACT.Identity, bias=bias[:, t : t + 1])
+                nc.vector.tensor_tensor(h[:, cols], second[:], biased[:], ALU.max)
+            return h
+
+        def place(t, h):
+            gain = gain_first[:] if t == 0 else gain_rest[:, t - 1, :]
+            nc.vector.tensor_tensor(page[t][:].indirect(list3[:]), h[:], gain, ALU.mult)
+
+        def fetch(t):
+            pair, e = divmod(t, 2)
+            for u in range(2):
+                nc.vector.tensor_copy(
+                    picked[pair][u][:, e, :],
+                    page[t][:].indirect(list4[:, u * HALF // 16 : (u + 1) * HALF // 16]),
+                )
+                if e == 1:
+                    nc.scalar.activation(
+                        x_bf16[u][:, :, 2 * pair : 2 * pair + 2],
+                        picked[pair][u][:].rearrange("p e c -> p c e"),
+                        ACT.Abs,
+                    )
+
+        h = readings(0)
+        for t in range(PACK):
+            place(t, h)
+            if t + 1 < PACK:
+                h = readings(t + 1)
+            if t == 0:
+                v2_codes = keep.tile([P, S2], U32, name="v2_codes", tag="gain_then_v2", align_bytes=64)
+                nc.vector.tensor_copy(v2_codes[:], table2[:].indirect(list2[:]))
+            fetch(t)
+
+        x_codes = held([P, OPENED], U32, "x_codes")
+        x_scale = held([P, OPENED], U8, "x_scale")
+        for u in range(2):
+            cols = slice(u * HALF, (u + 1) * HALF)
+            nc.vector.quantize_mx(
+                out=x_codes[:, cols].bitcast(FP8X4), scales=x_scale[:, cols],
+                in_=x_bf16[u][:].rearrange("p c t -> p (c t)"),
+            )
+
+        for i in range(S2 // P):
+            rows = slice(i * P, (i + 1) * P)
+            e_bank = psum.tile([P, BANK], F32, name="bank")
+            for u in range(2):
+                cols = slice(u * HALF, (u + 1) * HALF)
+                nc.tensor.matmul_mx(
+                    out=e_bank[:, cols], lhsT=v2_codes[:, rows].bitcast(FP8X4), lhsT_scale=v2_scales[:, rows],
+                    rhs=x_codes[:, cols].bitcast(FP8X4), rhs_scale=x_scale[:, cols], start=True, stop=True,
+                )
+            nc.vector.tensor_tensor(score[:, i, :], e_bank[:], score[:, i, :], ALU.add)
+            nc.scalar.activation(score[:, i, :], score[:, i, :], ACT.Tanh)
+            nc.sync.dma_start(out[rows, :], score[:, i, :])

@@ -23,6 +23,7 @@ QUADS = 4
 ROWS = 4
 BANK = 512
 HALF = OPENED // 2
+PIECE = S2 // 4
 
 
 def tile_list_lightbox_candidate_scores_kernel(
@@ -35,8 +36,8 @@ def tile_list_lightbox_candidate_scores_kernel(
         ring = ctx.enter_context(tc.tile_pool(name="ring", bufs=2))
         psum = ctx.enter_context(tc.psum_pool(name="psum", bufs=8))
 
-        def held(shape, dtype, name):
-            return keep.tile(shape, dtype, name=name, align_bytes=64)
+        def held(shape, dtype, name, tag=None):
+            return keep.tile(shape, dtype, name=name, tag=tag or name, align_bytes=64)
 
         list1 = keep.tile([P, S // 16], U16, name="list1")
         list2 = keep.tile([P, S2 // 16], U16, name="list2")
@@ -77,18 +78,46 @@ def tile_list_lightbox_candidate_scores_kernel(
             )
         w4_raw = held([P, PASSES, 2 * H], U8, "w4_raw")
         nc.sync.dma_start(w4_raw[:].bitcast(I32), w4_words.rearrange("a p n -> p a n").bitcast(I32))
+        staged = held([P, S + H + S2], U8, "staged")
+
+        def deal_rows(a):
+            for q in range(QUADS):
+                row = first_row + 16 * a + ROWS * q
+                nc.sync.dma_start(
+                    planes[a][32 * q : 32 * q + ROWS, :].bitcast(I32),
+                    staged[row : row + ROWS, 0 : plane_widths[a]].bitcast(I32),
+                )
+
         table = [held([P, T], U32, f"table{a}") for a in range(PASSES)]
-        for a in range(PASSES):
+
+        def load_table(a, cols):
             nc.sync.dma_start(
-                table[a][:].bitcast(I32), tab_words[a].rearrange("p t i -> p (t i)").bitcast(I32)
+                table[a][:, cols].bitcast(I32), tab_words[a].rearrange("p t i -> p (t i)").bitcast(I32)[:, cols]
             )
+
+        load_table(0, slice(0, T // 2))
+        picked_scales = held([P, S], U8, "picked_scales")
+        nc.vector.tensor_copy(picked_scales[:], tab_scale_rows[:].indirect(list1[:]))
+        nc.vector.tensor_copy(
+            staged[:, S : S + H].rearrange("p (t m) -> p t m", t=PACK),
+            w4_scale_rows[:].rearrange("p (m t) -> p t m", t=PACK),
+        )
+        nc.vector.tensor_copy(staged[:, 0:S].bitcast(I32), picked_scales[:].bitcast(I32))
+        deal_rows(0)
+        load_table(0, slice(T // 2, T))
+        picked_scales2 = held([P, S2], U8, "picked_scales2")
+        nc.vector.tensor_copy(picked_scales2[:], tab2_scale_rows[:].indirect(list2[:]))
+        nc.vector.tensor_copy(staged[:, S + H : S + H + S2].bitcast(I32), picked_scales2[:].bitcast(I32))
+        deal_rows(1)
+        load_table(1, slice(0, T))
+
         nc.sync.dma_start(list3[:], offs3)
         bias = keep.tile([P, PACK], F32, name="bias")
         nc.sync.dma_start(bias[:], b1.rearrange("(p t) -> p t", t=PACK))
         page = [held([P, T2], F32, f"page{t}") for t in range(PACK)]
         page_rows = page0.rearrange("(p t) c -> t p c", t=PACK)
         nc.sync.dma_start(page[0][:], page_rows[0])
-        gain_first = keep.tile([P, S], F32, name="gain_first", tag="gain_then_v2", align_bytes=64)
+        gain_first = held([P, S], F32, "gain_first", "odd")
         gain_rest = held([P, PACK - 1, S], F32, "gain_rest")
         wgs_rows = wgs.rearrange("(p t) j -> p t j", t=PACK)
         for q in range(QUADS):
@@ -103,29 +132,6 @@ def tile_list_lightbox_candidate_scores_kernel(
             nc.sync.dma_start(page[t][:], page_rows[t])
         score = held([P, S2 // P, OPENED], F32, "score")
         nc.sync.dma_start(score[:], lic.rearrange("(i p) j -> p i j", p=P))
-
-        staged = held([P, S + H + S2], U8, "staged")
-
-        def deal_rows(a):
-            for q in range(QUADS):
-                row = first_row + 16 * a + ROWS * q
-                nc.gpsimd.dma_start(
-                    planes[a][32 * q : 32 * q + ROWS, :].bitcast(I32),
-                    staged[row : row + ROWS, 0 : plane_widths[a]].bitcast(I32),
-                )
-
-        picked_scales = held([P, S], U8, "picked_scales")
-        nc.vector.tensor_copy(picked_scales[:], tab_scale_rows[:].indirect(list1[:]))
-        nc.vector.tensor_copy(
-            staged[:, S : S + H].rearrange("p (t m) -> p t m", t=PACK),
-            w4_scale_rows[:].rearrange("p (m t) -> p t m", t=PACK),
-        )
-        nc.vector.tensor_copy(staged[:, 0:S].bitcast(I32), picked_scales[:].bitcast(I32))
-        deal_rows(0)
-        picked_scales2 = held([P, S2], U8, "picked_scales2")
-        nc.vector.tensor_copy(picked_scales2[:], tab2_scale_rows[:].indirect(list2[:]))
-        nc.vector.tensor_copy(staged[:, S + H : S + H + S2].bitcast(I32), picked_scales2[:].bitcast(I32))
-        deal_rows(1)
 
         w1_bf16 = [held([P, H * PACK], BF16, f"w1_bf16{a}") for a in range(PASSES)]
         for a in range(PASSES):
@@ -144,18 +150,19 @@ def tile_list_lightbox_candidate_scores_kernel(
             nc.vector.quantize_mx(out=w1_codes[a][:].bitcast(FP8X4), scales=w1_scale[a][:], in_=w1_bf16[a][:])
 
         v_codes = [held([P, S], U32, f"v_codes{a}") for a in range(PASSES)]
-        nc.vector.tensor_copy(v_codes[0][:], table[0][:].indirect(list1[:]))
-        for u in range(S // BANK):
-            nc.vector.tensor_copy(
-                v_codes[1][:, u * BANK : (u + 1) * BANK],
-                table[1][:].indirect(list1[:, u * BANK // 16 : (u + 1) * BANK // 16]),
-            )
+        for a in range(PASSES):
+            for u in range(S // BANK):
+                nc.vector.tensor_copy(
+                    v_codes[a][:, u * BANK : (u + 1) * BANK],
+                    table[a][:].indirect(list1[:, u * BANK // 16 : (u + 1) * BANK // 16]),
+                )
 
-        picked = [[held([P, 2, HALF], F32, f"picked{pair}{u}") for u in range(2)] for pair in range(2)]
+        picked_early = held([P, PACK - 1, OPENED], F32, "picked_early")
+        picked_last = [held([P, HALF], F32, f"picked_last{u}") for u in range(2)]
         x_bf16 = [held([P, HALF, PACK], BF16, f"x_bf16{u}") for u in range(2)]
 
-        def readings(t):
-            h = ring.tile([P, S], F32, name="h")
+        def readings(t, after_half=None):
+            h = held([P, S], F32, f"h{t}", "odd" if t % 2 else "even")
             rows = slice(t * P, (t + 1) * P)
             for u in range(S // BANK):
                 cols = slice(u * BANK, (u + 1) * BANK)
@@ -177,35 +184,51 @@ def tile_list_lightbox_candidate_scores_kernel(
                 biased = ring.tile([P, BANK], F32, name="biased")
                 nc.scalar.activation(biased[:], first[:], ACT.Identity, bias=bias[:, t : t + 1])
                 nc.vector.tensor_tensor(h[:, cols], second[:], biased[:], ALU.max)
+                if after_half:
+                    after_half(h, u)
             return h
 
         def place(t, h):
-            gain = gain_first[:] if t == 0 else gain_rest[:, t - 1, :]
-            nc.vector.tensor_tensor(page[t][:].indirect(list3[:]), h[:], gain, ALU.mult)
+            nc.vector.tensor_tensor(page[t][:].indirect(list3[:]), h[:], gain_rest[:, t - 1, :], ALU.mult)
+
+        def place_first(h, u):
+            cols = slice(u * BANK, (u + 1) * BANK)
+            nc.vector.tensor_tensor(
+                page[0][:].indirect(list3[:, u * BANK // 16 : (u + 1) * BANK // 16]),
+                h[:, cols], gain_first[:, cols], ALU.mult,
+            )
 
         def fetch(t):
-            pair, e = divmod(t, 2)
-            for u in range(2):
-                nc.vector.tensor_copy(
-                    picked[pair][u][:, e, :],
-                    page[t][:].indirect(list4[:, u * HALF // 16 : (u + 1) * HALF // 16]),
-                )
-                if e == 1:
-                    nc.scalar.activation(
-                        x_bf16[u][:, :, 2 * pair : 2 * pair + 2],
-                        picked[pair][u][:].rearrange("p e c -> p c e"),
-                        ACT.Abs,
-                    )
+            nc.vector.tensor_copy(picked_early[:, t, :], page[t][:].indirect(list4[:]))
 
-        h = readings(0)
-        for t in range(PACK):
+        def fetch_last(u):
+            nc.vector.tensor_copy(
+                picked_last[u][:], page[PACK - 1][:].indirect(list4[:, u * HALF // 16 : (u + 1) * HALF // 16])
+            )
+            nc.scalar.activation(x_bf16[u][:, :, PACK - 1], picked_last[u][:], ACT.Abs)
+
+        def candidates(piece, tag):
+            codes = held([P, PIECE], U32, f"v2_codes{piece}", tag)
+            nc.vector.tensor_copy(
+                codes[:], table2[:].indirect(list2[:, piece * PIECE // 16 : (piece + 1) * PIECE // 16])
+            )
+            return codes
+
+        readings(0, place_first)
+        for t in range(1, PACK):
+            h = readings(t)
+            fetch(t - 1)
             place(t, h)
-            if t + 1 < PACK:
-                h = readings(t + 1)
-            if t == 0:
-                v2_codes = keep.tile([P, S2], U32, name="v2_codes", tag="gain_then_v2", align_bytes=64)
-                nc.vector.tensor_copy(v2_codes[:], table2[:].indirect(list2[:]))
-            fetch(t)
+        for u in range(2):
+            nc.scalar.activation(
+                x_bf16[u][:, :, 0 : PACK - 1],
+                picked_early[:, :, u * HALF : (u + 1) * HALF].rearrange("p t c -> p c t"),
+                ACT.Abs,
+            )
+        v2_codes = [candidates(0, "page2")]
+        for u in range(2):
+            fetch_last(u)
+        v2_codes.append(candidates(1, "odd"))
 
         x_codes = held([P, OPENED], U32, "x_codes")
         x_scale = held([P, OPENED], U8, "x_scale")
@@ -215,16 +238,21 @@ def tile_list_lightbox_candidate_scores_kernel(
                 out=x_codes[:, cols].bitcast(FP8X4), scales=x_scale[:, cols],
                 in_=x_bf16[u][:].rearrange("p c t -> p (c t)"),
             )
+            v2_codes.append(candidates(2 + u, f"picked_last{u}"))
 
         for i in range(S2 // P):
             rows = slice(i * P, (i + 1) * P)
+            piece, within = divmod(i * P, PIECE)
             e_bank = psum.tile([P, BANK], F32, name="bank")
             for u in range(2):
                 cols = slice(u * HALF, (u + 1) * HALF)
                 nc.tensor.matmul_mx(
-                    out=e_bank[:, cols], lhsT=v2_codes[:, rows].bitcast(FP8X4), lhsT_scale=v2_scales[:, rows],
+                    out=e_bank[:, cols], lhsT=v2_codes[piece][:, within : within + P].bitcast(FP8X4),
+                    lhsT_scale=v2_scales[:, rows],
                     rhs=x_codes[:, cols].bitcast(FP8X4), rhs_scale=x_scale[:, cols], start=True, stop=True,
                 )
-            nc.vector.tensor_tensor(score[:, i, :], e_bank[:], score[:, i, :], ALU.add)
-            nc.scalar.activation(score[:, i, :], score[:, i, :], ACT.Tanh)
-            nc.sync.dma_start(out[rows, :], score[:, i, :])
+            last = i == S2 // P - 1
+            for cols in [slice(0, HALF), slice(HALF, OPENED)] if last else [slice(0, OPENED)]:
+                nc.vector.tensor_tensor(score[:, i, cols], e_bank[:, cols], score[:, i, cols], ALU.add)
+                nc.scalar.activation(score[:, i, cols], score[:, i, cols], ACT.Tanh)
+                nc.sync.dma_start(out[rows, cols], score[:, i, cols])

@@ -47,11 +47,10 @@ def tile_list_lightbox_candidate_scores_kernel(
         tab_scale_rows = held([P, T], U8, "tab_scale_rows")
         tab2_scale_rows = held([P, T3], U8, "tab2_scale_rows")
         w4_scale_rows = held([P, H], U8, "w4_scale_rows")
-        plane_widths = [S + H, S + H + S2]
-        planes = [held([P, plane_widths[a]], U8, f"planes{a}") for a in range(PASSES)]
+        planes = [held([P, S + H], U8, f"planes{a}") for a in range(PASSES)]
         v_scales = [planes[a][:, 0:S] for a in range(PASSES)]
         w4_scale = [planes[a][:, S : S + H] for a in range(PASSES)]
-        v2_scales = planes[1][:, S + H : S + H + S2]
+        v2_scales = held([P, S2], U8, "v2_scales")
         first_row = P - PASSES * 16
         first_row2 = P - 16
         nc.vector.memset(tab_scale_rows[0:first_row, :].bitcast(I32), 0)
@@ -59,6 +58,7 @@ def tile_list_lightbox_candidate_scores_kernel(
         nc.vector.memset(tab2_scale_rows[0:first_row2, :].bitcast(I32), 0)
         for a in range(PASSES):
             nc.vector.memset(planes[a][:].bitcast(I32), 0)
+        nc.vector.memset(v2_scales[:].bitcast(I32), 0)
 
         nc.sync.dma_start(list1[:], offs)
         nc.sync.dma_start(
@@ -78,24 +78,44 @@ def tile_list_lightbox_candidate_scores_kernel(
             )
         w4_raw = held([P, PASSES, 2 * H], U8, "w4_raw")
         nc.sync.dma_start(w4_raw[:].bitcast(I32), w4_words.rearrange("a p n -> p a n").bitcast(I32))
-        staged = held([P, S + H + S2], U8, "staged")
+        table = [held([P, T], U32, f"table{a}") for a in range(PASSES)]
+        for a in range(PASSES):
+            nc.sync.dma_start(table[a][:].bitcast(I32), tab_words[a].rearrange("p t i -> p (t i)").bitcast(I32))
+        nc.sync.dma_start(list3[:], offs3)
+        bias = keep.tile([P, PACK], F32, name="bias")
+        nc.sync.dma_start(bias[:], b1.rearrange("(p t) -> p t", t=PACK))
+        page = [held([P, T2], F32, f"page{t}") for t in range(PACK)]
+        page_rows = page0.rearrange("(p t) c -> t p c", t=PACK)
+        nc.sync.dma_start(page[0][:], page_rows[0])
+        wgs_rows = wgs.rearrange("(p t) j -> p t j", t=PACK)
 
-        def deal_rows(a):
-            for q in range(QUADS):
-                row = first_row + 16 * a + ROWS * q
-                nc.sync.dma_start(
-                    planes[a][32 * q : 32 * q + ROWS, :].bitcast(I32),
-                    staged[row : row + ROWS, 0 : plane_widths[a]].bitcast(I32),
+        def load_gain(tile, slices):
+            for q in (0, 2, 1, 3):
+                nc.sync.dma_start(tile[32 * q : 32 * (q + 1), :, :], wgs_rows[:, slices, :])
+
+        gain_first = held([P, 1, S], F32, "gain_first", "odd")
+        load_gain(gain_first, slice(0, 1))
+        nc.sync.dma_start(list4[:], offs4)
+        nc.sync.dma_start(page[1][:], page_rows[1])
+        gain_second = held([P, 1, S], F32, "gain_second")
+        load_gain(gain_second, slice(1, 2))
+        nc.sync.dma_start(page[2][:], page_rows[2])
+        gain_rest = held([P, 2, S], F32, "gain_rest")
+        load_gain(gain_rest, slice(2, PACK))
+        nc.sync.dma_start(page[3][:], page_rows[3])
+        gain = [gain_first[:, 0, :], gain_second[:, 0, :], gain_rest[:, 0, :], gain_rest[:, 1, :]]
+        table2 = held([P, T3], U32, "table2")
+        nc.sync.dma_start(table2[:].bitcast(I32), tab2_words[0].rearrange("p t i -> p (t i)").bitcast(I32))
+        score = held([P, S2 // P, OPENED], F32, "score")
+        nc.sync.dma_start(score[:], lic.rearrange("(i p) j -> p i j", p=P))
+
+        def deal_rows(plane, source, first):
+            for r in range(ROWS):
+                nc.gpsimd.dma_start(
+                    plane[r:P:32, :].bitcast(I32), source[first + r : first + 16 : ROWS, :].bitcast(I32)
                 )
 
-        table = [held([P, T], U32, f"table{a}") for a in range(PASSES)]
-
-        def load_table(a, cols):
-            nc.sync.dma_start(
-                table[a][:, cols].bitcast(I32), tab_words[a].rearrange("p t i -> p (t i)").bitcast(I32)[:, cols]
-            )
-
-        load_table(0, slice(0, T // 2))
+        staged = held([P, S + H], U8, "staged")
         picked_scales = held([P, S], U8, "picked_scales")
         nc.vector.tensor_copy(picked_scales[:], tab_scale_rows[:].indirect(list1[:]))
         nc.vector.tensor_copy(
@@ -103,51 +123,33 @@ def tile_list_lightbox_candidate_scores_kernel(
             w4_scale_rows[:].rearrange("p (m t) -> p t m", t=PACK),
         )
         nc.vector.tensor_copy(staged[:, 0:S].bitcast(I32), picked_scales[:].bitcast(I32))
-        deal_rows(0)
-        load_table(0, slice(T // 2, T))
+        for a in range(PASSES):
+            deal_rows(planes[a], staged, first_row + 16 * a)
         picked_scales2 = held([P, S2], U8, "picked_scales2")
         nc.vector.tensor_copy(picked_scales2[:], tab2_scale_rows[:].indirect(list2[:]))
-        nc.vector.tensor_copy(staged[:, S + H : S + H + S2].bitcast(I32), picked_scales2[:].bitcast(I32))
-        deal_rows(1)
-        load_table(1, slice(0, T))
+        deal_rows(v2_scales, picked_scales2, first_row2)
 
-        nc.sync.dma_start(list3[:], offs3)
-        bias = keep.tile([P, PACK], F32, name="bias")
-        nc.sync.dma_start(bias[:], b1.rearrange("(p t) -> p t", t=PACK))
-        page = [held([P, T2], F32, f"page{t}") for t in range(PACK)]
-        page_rows = page0.rearrange("(p t) c -> t p c", t=PACK)
-        nc.sync.dma_start(page[0][:], page_rows[0])
-        gain_first = held([P, S], F32, "gain_first", "odd")
-        gain_rest = held([P, PACK - 1, S], F32, "gain_rest")
-        wgs_rows = wgs.rearrange("(p t) j -> p t j", t=PACK)
-        for q in range(QUADS):
-            nc.sync.dma_start(gain_first[32 * q : 32 * (q + 1), :], wgs_rows[:, 0, :])
-        table2 = held([P, T3], U32, "table2")
-        nc.sync.dma_start(table2[:].bitcast(I32), tab2_words[0].rearrange("p t i -> p (t i)").bitcast(I32))
-        nc.sync.dma_start(page[1][:], page_rows[1])
-        for q in range(QUADS):
-            nc.sync.dma_start(gain_rest[32 * q : 32 * (q + 1), :, :], wgs_rows[:, 1:PACK, :])
-        nc.sync.dma_start(list4[:], offs4)
-        for t in range(2, PACK):
-            nc.sync.dma_start(page[t][:], page_rows[t])
-        score = held([P, S2 // P, OPENED], F32, "score")
-        nc.sync.dma_start(score[:], lic.rearrange("(i p) j -> p i j", p=P))
-
-        w1_bf16 = [held([P, H * PACK], BF16, f"w1_bf16{a}") for a in range(PASSES)]
-        for a in range(PASSES):
+        w1_parts = [(pair, a) for pair in range(2) for a in range(PASSES)]
+        w1_bf16 = {}
+        for pair, a in w1_parts:
+            w1_bf16[pair, a] = held([P, 2, P, PACK], BF16, f"w1_bf16{pair}{a}")
             nc.scalar.copy(
-                w1_bf16[a][:].rearrange("p (t m j) -> p m t j", t=PACK, j=PACK),
-                w1_raw[a][:].rearrange("p j (m t) -> p m t j", t=PACK),
+                w1_bf16[pair, a][:],
+                w1_raw[a][:].rearrange("p j (m t) -> p t m j", t=PACK)[:, 2 * pair : 2 * pair + 2, :, :],
             )
         w4_codes = held([P, PASSES, 2 * H], U8, "w4_codes")
         nc.vector.tensor_copy(
             w4_codes[:].bitcast(U16).rearrange("p a (t m) -> p a t m", t=PACK),
             w4_raw[:].bitcast(U16).rearrange("p a (m t) -> p a t m", t=PACK),
         )
-        w1_codes = [held([P, H], U32, f"w1_codes{a}") for a in range(PASSES)]
-        w1_scale = [held([P, H], U8, f"w1_scale{a}") for a in range(PASSES)]
-        for a in range(PASSES):
-            nc.vector.quantize_mx(out=w1_codes[a][:].bitcast(FP8X4), scales=w1_scale[a][:], in_=w1_bf16[a][:])
+        w1_codes, w1_scale = {}, {}
+        for pair, a in w1_parts:
+            w1_codes[pair, a] = held([P, 2 * P], U32, f"w1_codes{pair}{a}")
+            w1_scale[pair, a] = held([P, 2 * P], U8, f"w1_scale{pair}{a}")
+            nc.vector.quantize_mx(
+                out=w1_codes[pair, a][:].bitcast(FP8X4), scales=w1_scale[pair, a][:],
+                in_=w1_bf16[pair, a][:].rearrange("p e m j -> p (e m j)"),
+            )
 
         v_codes = [held([P, S], U32, f"v_codes{a}") for a in range(PASSES)]
         for a in range(PASSES):
@@ -164,6 +166,7 @@ def tile_list_lightbox_candidate_scores_kernel(
         def readings(t, after_half=None):
             h = held([P, S], F32, f"h{t}", "odd" if t % 2 else "even")
             rows = slice(t * P, (t + 1) * P)
+            rows_in_pair = slice(t % 2 * P, (t % 2 + 1) * P)
             for u in range(S // BANK):
                 cols = slice(u * BANK, (u + 1) * BANK)
                 first = psum.tile([P, BANK], F32, name="bank")
@@ -174,8 +177,8 @@ def tile_list_lightbox_candidate_scores_kernel(
                         start=a == 0, stop=a == PASSES - 1,
                     )
                     nc.tensor.matmul_mx(
-                        out=first[:], lhsT=w1_codes[a][:, rows].bitcast(FP8X4),
-                        lhsT_scale=w1_scale[a][:, rows], **moving,
+                        out=first[:], lhsT=w1_codes[t // 2, a][:, rows_in_pair].bitcast(FP8X4),
+                        lhsT_scale=w1_scale[t // 2, a][:, rows_in_pair], **moving,
                     )
                     nc.tensor.matmul_mx(
                         out=second[:], lhsT=w4_codes[:, a, 2 * t * P : 2 * (t + 1) * P].bitcast(FP4X4),
@@ -189,13 +192,13 @@ def tile_list_lightbox_candidate_scores_kernel(
             return h
 
         def place(t, h):
-            nc.vector.tensor_tensor(page[t][:].indirect(list3[:]), h[:], gain_rest[:, t - 1, :], ALU.mult)
+            nc.vector.tensor_tensor(page[t][:].indirect(list3[:]), h[:], gain[t], ALU.mult)
 
         def place_first(h, u):
             cols = slice(u * BANK, (u + 1) * BANK)
             nc.vector.tensor_tensor(
                 page[0][:].indirect(list3[:, u * BANK // 16 : (u + 1) * BANK // 16]),
-                h[:, cols], gain_first[:, cols], ALU.mult,
+                h[:, cols], gain[0][:, cols], ALU.mult,
             )
 
         def fetch(t):

@@ -89,29 +89,25 @@ def tile_list_lightbox_candidate_scores_kernel(
         nc.sync.dma_start(page[0][:], page_rows[0])
         wgs_rows = wgs.rearrange("(p t) j -> p t j", t=PACK)
 
-        def load_gain(tile, slices):
+        def load_gain(tile, t, cols):
             for q in (0, 2, 1, 3):
-                nc.sync.dma_start(tile[32 * q : 32 * (q + 1), :, :], wgs_rows[:, slices, :])
+                nc.sync.dma_start(tile[32 * q : 32 * (q + 1), cols], wgs_rows[:, t, cols])
 
-        gain_first = held([P, 1, S], F32, "gain_first", "odd")
-        load_gain(gain_first, slice(0, 1))
+        gain = [held([P, S], F32, f"gain{t}", "odd" if t == 0 else None) for t in range(PACK)]
+        for u in range(S // BANK):
+            load_gain(gain[0], 0, slice(u * BANK, (u + 1) * BANK))
         nc.sync.dma_start(list4[:], offs4)
-        nc.sync.dma_start(page[1][:], page_rows[1])
-        gain_second = held([P, 1, S], F32, "gain_second")
-        load_gain(gain_second, slice(1, 2))
-        nc.sync.dma_start(page[2][:], page_rows[2])
-        gain_rest = held([P, 2, S], F32, "gain_rest")
-        load_gain(gain_rest, slice(2, PACK))
-        nc.sync.dma_start(page[3][:], page_rows[3])
-        gain = [gain_first[:, 0, :], gain_second[:, 0, :], gain_rest[:, 0, :], gain_rest[:, 1, :]]
+        for t in range(1, PACK):
+            nc.sync.dma_start(page[t][:], page_rows[t])
+            load_gain(gain[t], t, slice(0, S))
         table2 = held([P, T3], U32, "table2")
         nc.sync.dma_start(table2[:].bitcast(I32), tab2_words[0].rearrange("p t i -> p (t i)").bitcast(I32))
         score = held([P, S2 // P, OPENED], F32, "score")
         nc.sync.dma_start(score[:], lic.rearrange("(i p) j -> p i j", p=P))
 
-        def deal_rows(plane, source, first):
+        def deal_rows(queue, plane, source, first):
             for r in range(ROWS):
-                nc.gpsimd.dma_start(
+                queue.dma_start(
                     plane[r:P:32, :].bitcast(I32), source[first + r : first + 16 : ROWS, :].bitcast(I32)
                 )
 
@@ -123,17 +119,18 @@ def tile_list_lightbox_candidate_scores_kernel(
             w4_scale_rows[:].rearrange("p (m t) -> p t m", t=PACK),
         )
         nc.vector.tensor_copy(staged[:, 0:S].bitcast(I32), picked_scales[:].bitcast(I32))
-        for a in range(PASSES):
-            deal_rows(planes[a], staged, first_row + 16 * a)
+        for a, queue in enumerate((nc.scalar, nc.gpsimd)):
+            deal_rows(queue, planes[a], staged, first_row + 16 * a)
         picked_scales2 = held([P, S2], U8, "picked_scales2")
         nc.vector.tensor_copy(picked_scales2[:], tab2_scale_rows[:].indirect(list2[:]))
-        deal_rows(v2_scales, picked_scales2, first_row2)
+        deal_rows(nc.gpsimd, v2_scales, picked_scales2, first_row2)
 
         w1_parts = [(pair, a) for pair in range(2) for a in range(PASSES)]
         w1_bf16 = {}
         for pair, a in w1_parts:
             w1_bf16[pair, a] = held([P, 2, P, PACK], BF16, f"w1_bf16{pair}{a}")
-            nc.scalar.copy(
+            cast = nc.scalar.copy if pair == 0 else nc.vector.tensor_copy
+            cast(
                 w1_bf16[pair, a][:],
                 w1_raw[a][:].rearrange("p j (m t) -> p t m j", t=PACK)[:, 2 * pair : 2 * pair + 2, :, :],
             )
@@ -192,7 +189,7 @@ def tile_list_lightbox_candidate_scores_kernel(
             return h
 
         def place(t, h):
-            nc.vector.tensor_tensor(page[t][:].indirect(list3[:]), h[:], gain[t], ALU.mult)
+            nc.vector.tensor_tensor(page[t][:].indirect(list3[:]), h[:], gain[t][:], ALU.mult)
 
         def place_first(h, u):
             cols = slice(u * BANK, (u + 1) * BANK)
@@ -243,19 +240,19 @@ def tile_list_lightbox_candidate_scores_kernel(
             )
             v2_codes.append(candidates(2 + u, f"picked_last{u}"))
 
+        halves = [slice(0, HALF), slice(HALF, OPENED)]
+        whole = [slice(0, OPENED)]
         for i in range(S2 // P):
             rows = slice(i * P, (i + 1) * P)
             piece, within = divmod(i * P, PIECE)
             e_bank = psum.tile([P, BANK], F32, name="bank")
-            for u in range(2):
-                cols = slice(u * HALF, (u + 1) * HALF)
+            for cols in halves if i == 0 else whole:
                 nc.tensor.matmul_mx(
                     out=e_bank[:, cols], lhsT=v2_codes[piece][:, within : within + P].bitcast(FP8X4),
                     lhsT_scale=v2_scales[:, rows],
                     rhs=x_codes[:, cols].bitcast(FP8X4), rhs_scale=x_scale[:, cols], start=True, stop=True,
                 )
-            last = i == S2 // P - 1
-            for cols in [slice(0, HALF), slice(HALF, OPENED)] if last else [slice(0, OPENED)]:
+            for cols in halves if i == S2 // P - 1 else whole:
                 nc.vector.tensor_tensor(score[:, i, cols], e_bank[:, cols], score[:, i, cols], ALU.add)
                 nc.scalar.activation(score[:, i, cols], score[:, i, cols], ACT.Tanh)
                 nc.sync.dma_start(out[rows, cols], score[:, i, cols])

from contextlib import ExitStack

import concourse.mybir as mybir

K, H, T, S, T2, T3, S2, OPENED = 1024, 512, 4096, 1024, 2048, 2048, 1024, 512
FLOPS = 2 * (2 * K * H * S + H * S2 * OPENED)

F32 = mybir.dt.float32
BF16 = mybir.dt.bfloat16
I32 = mybir.dt.int32
U32 = mybir.dt.uint32
U16 = mybir.dt.uint16
U8 = mybir.dt.uint8
FP8X4 = mybir.dt.float8_e4m3fn_x4
FP4X4 = mybir.dt.float4_e2m1fn_x4
ALU = mybir.AluOpType
ACT = mybir.ActivationFunctionType

P = 128
PACK = 4
PASSES = K // (P * PACK)
QUADS = 4
ROWS = 4
BANK = 512
HALF = OPENED // 2
PIECE = S2 // 4


def tile_list_lightbox_candidate_scores_kernel(
    tc, tab_words, tab_scales, tab2_words, tab2_scales, offs, offs2, offs3, offs4,
    w1, b1, w4_words, w4_scales, page0, wgs, lic, out,
):
    nc = tc.nc
    with ExitStack() as ctx:
        keep = ctx.enter_context(tc.tile_pool(name="keep", bufs=1))
        ring = ctx.enter_context(tc.tile_pool(name="ring", bufs=2))
        psum = ctx.enter_context(tc.psum_pool(name="psum", bufs=8))

        def held(shape, dtype, name, tag=None):
            return keep.tile(shape, dtype, name=name, tag=tag or name, align_bytes=64)

        list1 = keep.tile([P, S // 16], U16, name="list1")
        list2 = keep.tile([P, S2 // 16], U16, name="list2")
        list3 = keep.tile([P, S // 16], U16, name="list3")
        list4 = keep.tile([P, OPENED // 16], U16, name="list4")

        tab_scale_rows = held([P, T], U8, "tab_scale_rows")
        tab2_scale_rows = held([P, T3], U8, "tab2_scale_rows")
        w4_scale_rows = held([P, H], U8, "w4_scale_rows")
        planes = [held([P, S + H], U8, f"planes{a}") for a in range(PASSES)]
        v_scales = [planes[a][:, 0:S] for a in range(PASSES)]
        w4_scale = [planes[a][:, S : S + H] for a in range(PASSES)]
        v2_scales = held([P, S2], U8, "v2_scales")
        first_row = P - PASSES * 16
        first_row2 = P - 16
        nc.vector.memset(tab_scale_rows[0:first_row, :].bitcast(I32), 0)
        nc.vector.memset(w4_scale_rows[0:first_row, :].bitcast(I32), 0)
        nc.vector.memset(tab2_scale_rows[0:first_row2, :].bitcast(I32), 0)
        for a in range(PASSES):
            nc.vector.memset(planes[a][:].bitcast(I32), 0)
        nc.vector.memset(v2_scales[:].bitcast(I32), 0)

        nc.sync.dma_start(list1[:], offs)
        nc.sync.dma_start(
            tab_scale_rows[first_row:P, :].bitcast(I32),
            tab_scales.rearrange("a q t -> (a q) t").bitcast(I32),
        )
        nc.sync.dma_start(
            w4_scale_rows[first_row:P, :].bitcast(I32),
            w4_scales.rearrange("a q c -> (a q) c").bitcast(I32),
        )
        nc.sync.dma_start(list2[:], offs2)
        nc.sync.dma_start(tab2_scale_rows[first_row2:P, :].bitcast(I32), tab2_scales[0].bitcast(I32))
        w1_raw = [held([P, PACK, H], F32, f"w1_raw{a}") for a in range(PASSES)]
        for a in range(PASSES):
            nc.sync.dma_start(
                w1_raw[a][:], w1[a * P * PACK : (a + 1) * P * PACK, :].rearrange("(p j) c -> p j c", j=PACK)
            )
        w4_raw = held([P, PASSES, 2 * H], U8, "w4_raw")
        nc.sync.dma_start(w4_raw[:].bitcast(I32), w4_words.rearrange("a p n -> p a n").bitcast(I32))
        table = [held([P, T], U32, f"table{a}") for a in range(PASSES)]
        for a in range(PASSES):
            nc.sync.dma_start(table[a][:].bitcast(I32), tab_words[a].rearrange("p t i -> p (t i)").bitcast(I32))
        nc.sync.dma_start(list3[:], offs3)
        bias = keep.tile([P, PACK], F32, name="bias")
        nc.sync.dma_start(bias[:], b1.rearrange("(p t) -> p t", t=PACK))
        page = [held([P, T2], F32, f"page{t}") for t in range(PACK)]
        page_rows = page0.rearrange("(p t) c -> t p c", t=PACK)
        nc.sync.dma_start(page[0][:], page_rows[0])
        wgs_rows = wgs.rearrange("(p t) j -> p t j", t=PACK)

        def load_gain(tile, t, cols):
            for q in (0, 2, 1, 3):
                nc.sync.dma_start(tile[32 * q : 32 * (q + 1), cols], wgs_rows[:, t, cols])

        gain = [held([P, S], F32, f"gain{t}", "odd" if t == 0 else None) for t in range(PACK)]
        for u in range(S // BANK):
            load_gain(gain[0], 0, slice(u * BANK, (u + 1) * BANK))
        nc.sync.dma_start(list4[:], offs4)
        for t in range(1, PACK):
            nc.sync.dma_start(page[t][:], page_rows[t])
            load_gain(gain[t], t, slice(0, S))
        table2 = held([P, T3], U32, "table2")
        nc.sync.dma_start(table2[:].bitcast(I32), tab2_words[0].rearrange("p t i -> p (t i)").bitcast(I32))
        score = held([P, S2 // P, OPENED], F32, "score")
        nc.sync.dma_start(score[:], lic.rearrange("(i p) j -> p i j", p=P))

        def deal_rows(queue, plane, source, first):
            for r in range(ROWS):
                queue.dma_start(
                    plane[r:P:32, :].bitcast(I32), source[first + r : first + 16 : ROWS, :].bitcast(I32)
                )

        staged = held([P, S + H], U8, "staged")
        picked_scales = held([P, S], U8, "picked_scales")
        nc.vector.tensor_copy(picked_scales[:], tab_scale_rows[:].indirect(list1[:]))
        nc.vector.tensor_copy(
            staged[:, S : S + H].rearrange("p (t m) -> p t m", t=PACK),
            w4_scale_rows[:].rearrange("p (m t) -> p t m", t=PACK),
        )
        nc.vector.tensor_copy(staged[:, 0:S].bitcast(I32), picked_scales[:].bitcast(I32))
        for a, queue in enumerate((nc.scalar, nc.gpsimd)):
            deal_rows(queue, planes[a], staged, first_row + 16 * a)
        picked_scales2 = held([P, S2], U8, "picked_scales2")
        nc.vector.tensor_copy(picked_scales2[:], tab2_scale_rows[:].indirect(list2[:]))
        deal_rows(nc.gpsimd, v2_scales, picked_scales2, first_row2)

        w1_parts = [(pair, a) for pair in range(2) for a in range(PASSES)]
        w1_bf16 = {}
        for pair, a in w1_parts:
            w1_bf16[pair, a] = held([P, 2, P, PACK], BF16, f"w1_bf16{pair}{a}")
            cast = nc.scalar.copy if pair == 0 else nc.vector.tensor_copy
            cast(
                w1_bf16[pair, a][:],
                w1_raw[a][:].rearrange("p j (m t) -> p t m j", t=PACK)[:, 2 * pair : 2 * pair + 2, :, :],
            )
        w4_codes = held([P, PASSES, 2 * H], U8, "w4_codes")
        nc.vector.tensor_copy(
            w4_codes[:].bitcast(U16).rearrange("p a (t m) -> p a t m", t=PACK),
            w4_raw[:].bitcast(U16).rearrange("p a (m t) -> p a t m", t=PACK),
        )
        w1_codes, w1_scale = {}, {}
        for pair, a in w1_parts:
            w1_codes[pair, a] = held([P, 2 * P], U32, f"w1_codes{pair}{a}")
            w1_scale[pair, a] = held([P, 2 * P], U8, f"w1_scale{pair}{a}")
            nc.vector.quantize_mx(
                out=w1_codes[pair, a][:].bitcast(FP8X4), scales=w1_scale[pair, a][:],
                in_=w1_bf16[pair, a][:].rearrange("p e m j -> p (e m j)"),
            )

        v_codes = [held([P, S], U32, f"v_codes{a}") for a in range(PASSES)]
        for a in range(PASSES):
            for u in range(S // BANK):
                nc.vector.tensor_copy(
                    v_codes[a][:, u * BANK : (u + 1) * BANK],
                    table[a][:].indirect(list1[:, u * BANK // 16 : (u + 1) * BANK // 16]),
                )

        picked_early = held([P, PACK - 1, OPENED], F32, "picked_early")
        picked_last = [held([P, HALF], F32, f"picked_last{u}") for u in range(2)]
        x_bf16 = [held([P, HALF, PACK], BF16, f"x_bf16{u}") for u in range(2)]

        def readings(t, after_half=None):
            h = held([P, S], F32, f"h{t}", "odd" if t % 2 else "even")
            rows = slice(t * P, (t + 1) * P)
            rows_in_pair = slice(t % 2 * P, (t % 2 + 1) * P)
            for u in range(S // BANK):
                cols = slice(u * BANK, (u + 1) * BANK)
                first = psum.tile([P, BANK], F32, name="bank")
                second = psum.tile([P, BANK], F32, name="bank")
                for a in range(PASSES):
                    moving = dict(
                        rhs=v_codes[a][:, cols].bitcast(FP8X4), rhs_scale=v_scales[a][:, cols],
                        start=a == 0, stop=a == PASSES - 1,
                    )
                    nc.tensor.matmul_mx(
                        out=first[:], lhsT=w1_codes[t // 2, a][:, rows_in_pair].bitcast(FP8X4),
                        lhsT_scale=w1_scale[t // 2, a][:, rows_in_pair], **moving,
                    )
                    nc.tensor.matmul_mx(
                        out=second[:], lhsT=w4_codes[:, a, 2 * t * P : 2 * (t + 1) * P].bitcast(FP4X4),
                        lhsT_scale=w4_scale[a][:, rows], **moving,
                    )
                biased = ring.tile([P, BANK], F32, name="biased")
                nc.scalar.activation(biased[:], first[:], ACT.Identity, bias=bias[:, t : t + 1])
                nc.vector.tensor_tensor(h[:, cols], second[:], biased[:], ALU.max)
                if after_half:
                    after_half(h, u)
            return h

        def place(t, h):
            nc.vector.tensor_tensor(page[t][:].indirect(list3[:]), h[:], gain[t][:], ALU.mult)

        def place_first(h, u):
            cols = slice(u * BANK, (u + 1) * BANK)
            nc.vector.tensor_tensor(
                page[0][:].indirect(list3[:, u * BANK // 16 : (u + 1) * BANK // 16]),
                h[:, cols], gain[0][:, cols], ALU.mult,
            )

        def fetch(t):
            nc.vector.tensor_copy(picked_early[:, t, :], page[t][:].indirect(list4[:]))

        def fetch_last(u):
            nc.vector.tensor_copy(
                picked_last[u][:], page[PACK - 1][:].indirect(list4[:, u * HALF // 16 : (u + 1) * HALF // 16])
            )
            nc.scalar.activation(x_bf16[u][:, :, PACK - 1], picked_last[u][:], ACT.Abs)

        def candidates(piece, tag):
            codes = held([P, PIECE], U32, f"v2_codes{piece}", tag)
            nc.vector.tensor_copy(
                codes[:], table2[:].indirect(list2[:, piece * PIECE // 16 : (piece + 1) * PIECE // 16])
            )
            return codes

        readings(0, place_first)
        for t in range(1, PACK):
            h = readings(t)
            fetch(t - 1)
            place(t, h)
        for u in range(2):
            nc.scalar.activation(
                x_bf16[u][:, :, 0 : PACK - 1],
                picked_early[:, :, u * HALF : (u + 1) * HALF].rearrange("p t c -> p c t"),
                ACT.Abs,
            )
        v2_codes = [candidates(0, "page2")]
        for u in range(2):
            fetch_last(u)
        v2_codes.append(candidates(1, "odd"))

        x_codes = held([P, OPENED], U32, "x_codes")
        x_scale = held([P, OPENED], U8, "x_scale")
        for u in range(2):
            cols = slice(u * HALF, (u + 1) * HALF)
            nc.vector.quantize_mx(
                out=x_codes[:, cols].bitcast(FP8X4), scales=x_scale[:, cols],
                in_=x_bf16[u][:].rearrange("p c t -> p (c t)"),
            )
            v2_codes.append(candidates(2 + u, f"picked_last{u}"))

        halves = [slice(0, HALF), slice(HALF, OPENED)]
        whole = [slice(0, OPENED)]
        for i in range(S2 // P):
            rows = slice(i * P, (i + 1) * P)
            piece, within = divmod(i * P, PIECE)
            e_bank = psum.tile([P, BANK], F32, name="bank")
            for cols in halves if i == 0 else whole:
                nc.tensor.matmul_mx(
                    out=e_bank[:, cols], lhsT=v2_codes[piece][:, within : within + P].bitcast(FP8X4),
                    lhsT_scale=v2_scales[:, rows],
                    rhs=x_codes[:, cols].bitcast(FP8X4), rhs_scale=x_scale[:, cols], start=True, stop=True,
                )
            for cols in halves if i == S2 // P - 1 else whole:
                nc.vector.tensor_tensor(score[:, i, cols], e_bank[:, cols], score[:, i, cols], ALU.add)
                nc.scalar.activation(score[:, i, cols], score[:, i, cols], ACT.Tanh)
                nc.sync.dma_start(out[rows, cols], score[:, i, cols])
